import numpy as np
import ml_dtypes


def mxq(x, axis, fmt="e4m3"):
    dtype, down = {"e4m3": (ml_dtypes.float8_e4m3fn, 7), "e5m2": (ml_dtypes.float8_e5m2, 14)}[fmt]
    v = np.moveaxis(np.asarray(x, np.float32).astype(ml_dtypes.bfloat16).astype(np.float64), axis, -1)
    blocks = v.reshape(v.shape[:-1] + (-1, 32))
    amax = np.abs(blocks).max(-1, keepdims=True)
    byte = np.maximum(np.where(amax > 0, np.frexp(amax)[1] - 1 + 127, 0) - down, 1)
    scale = np.exp2(byte - 127.0)
    codes = (blocks / scale).astype(np.float32).astype(dtype).astype(np.float64)
    return np.moveaxis((codes * scale).reshape(v.shape), -1, axis)


WIDE = False


def mx_kscale(k):
    if not WIDE:
        return np.ones(k)
    levels = np.array([10, -10, 5, -5, 0])
    if k % 512:
        return np.exp2(np.random.permutation(np.resize(levels, k // 32))).repeat(32)
    a = np.empty((k // 512, 16))
    for p in range(k // 512):
        a[p, :8] = np.random.permutation(np.resize(levels, 8))
        for g in range(8):
            far = levels[np.abs(levels - a[p, g]) >= 10]
            a[p, g + 8] = far[np.random.randint(len(far))]
    return np.exp2(a.ravel()).repeat(32)


BF16 = ml_dtypes.bfloat16


def bf(x):
    return np.asarray(x, np.float32).astype(BF16)


def f64(x):
    return np.asarray(x).astype(np.float64)


B, H, C = 4096, 512, 2
HC = C * H


def draw0():
    s = mx_kscale(H)
    return {"z0": bf(np.random.standard_normal((B, H))),
            "g": bf((1.0 + 0.1 * np.random.standard_normal(H)) * s),
            "w": bf(np.random.standard_normal((H, HC)) / np.sqrt(H) / s[:, None]),
            "dx0": bf(np.random.standard_normal((B, C)) * np.sqrt(2.0 / C)),
            "dxm": bf(np.random.standard_normal((B, C)) * np.sqrt(2.0 / C))}


def vector_field(z, g, wq, channels):
    batch, hidden = z.shape
    u = z * g[None, :]
    f = np.tanh(mxq(u, 1, "e4m3") @ wq)
    return f.reshape(batch, channels, hidden)


def apply_control(f, dx):
    return np.sum(f * dx[:, :, None], axis=1)


def core(z0, g, w, dx0, dxm):
    z0, g, dx0, dxm = f64(z0), f64(g), f64(dx0), f64(dxm)
    channels = dx0.shape[1]
    wq = mxq(f64(w), 0, "e4m3")
    f0 = vector_field(z0, g, wq, channels)
    zmid = z0 + apply_control(f0, dx0)
    f1 = vector_field(zmid, g, wq, channels)
    return apply_control(f1, dxm)


def e4m3fn_bytes(y):
    return np.clip(np.asarray(y, np.float64), -448.0, 448.0).astype(np.float32).astype(ml_dtypes.float8_e4m3fn).view(np.uint8)


def e4m3fn_values(b):
    return np.asarray(b, np.uint8).view(ml_dtypes.float8_e4m3fn).astype(np.float64)


def setup_inputs():
    d = draw0()
    x0 = np.asarray(d['w']).astype(np.float64)
    s = (np.max(np.abs(x0), axis=(1,), keepdims=True) / 448.0).astype(np.float32)
    out = {}
    for k, v in d.items():
        if k == 'w':
            out['w_bytes'] = e4m3fn_bytes(x0 / s.astype(np.float64))
            out['w_scale'] = s
        else:
            out[k] = v
    return out


def reference(z0, g, w_bytes, w_scale, dx0, dxm):
    return core(z0, g, e4m3fn_values(w_bytes) * w_scale.astype(np.float64), dx0, dxm)

@@ -1,0 +1,229 @@
+from contextlib import ExitStack
+
+import concourse.mybir as mybir
+from concourse.masks import make_identity
+
+B, H, C = 4096, 512, 2
+HC = C * H
+P = 128
+PACK = 4
+TILES = B // P
+
+F32 = mybir.dt.float32
+BF16 = mybir.dt.bfloat16
+U32 = mybir.dt.uint32
+U8 = mybir.dt.uint8
+FP8 = mybir.dt.float8_e4m3fn
+FP8X4 = mybir.dt.float8_e4m3fn_x4
+ALU = mybir.AluOpType
+ACT = mybir.ActivationFunctionType
+
+FLOPS = 2 * 2 * B * H * HC
+
+Z_CHUNKS = (2, 2, 4, 8, 8, 8)
+GROUPS = TILES // 2
+
+
+def tile_neuralcdemidpointstep_t_kernel(tc, z0, g, w_bytes, w_scale, dx0, dxm, out):
+    nc = tc.nc
+    z_view = z0.rearrange("(p j) h -> p j h", j=TILES)
+    out_view = out.rearrange("(p j) h -> p j h", j=TILES)
+    wb_view = w_bytes.rearrange("(p t) n -> p t n", t=PACK)
+
+    with ExitStack() as ctx:
+        ctx.enter_context(tc.manual_schedule())
+        keep = ctx.enter_context(tc.tile_pool(name="keep", bufs=1))
+        work = ctx.enter_context(tc.tile_pool(name="work", bufs=6))
+        psum = ctx.enter_context(tc.psum_pool(name="psum", bufs=1))
+
+        wb = [keep.tile([P, PACK, H], U8, name="wb%d" % c, align_bytes=64) for c in range(C)]
+        wsc = keep.tile([P, PACK], F32, name="wsc")
+        g4 = keep.tile([P, PACK], BF16, name="g4")
+        gx = keep.tile([P, 2 * P, PACK], BF16, name="gx", align_bytes=64)
+        dx_raw = keep.tile([P, 2, TILES * C], BF16, name="dx_raw")
+        dx = keep.tile([P, 2, TILES * C], F32, name="dx")
+        ident = keep.tile([P, P], F32, name="ident")
+        warm = keep.tile([P, 1], F32, name="warm")
+
+        z_tiles = {}
+        nc.sync.dma_start(out=wb[0][:], in_=wb_view[:, :, 0:H])
+        nc.scalar.dma_start(out=wsc[:], in_=w_scale.rearrange("(p t) o -> p (t o)", t=PACK))
+        nc.scalar.dma_start(out=g4[:], in_=g.rearrange("(p t) -> p t", t=PACK))
+        nc.scalar.dma_start(out=dx_raw[:, 0, :], in_=dx0.rearrange("(p j) c -> p (j c)", j=TILES))
+        nc.scalar.dma_start(out=dx_raw[:, 1, :], in_=dxm.rearrange("(p j) c -> p (j c)", j=TILES))
+        j0 = 0
+        for k, n in enumerate(Z_CHUNKS):
+            zc = keep.tile([P, n, H], BF16, name="z%d" % k, align_bytes=64)
+            nc.sync.dma_start(out=zc[:], in_=z_view[:, j0 : j0 + n, :])
+            for i in range(n):
+                z_tiles[j0 + i] = zc[:, i, :]
+            j0 += n
+            if k == 0:
+                nc.sync.dma_start(out=wb[1][:], in_=wb_view[:, :, H:HC])
+
+        nc.vector.memset(warm[:], 0.0)
+        nc.scalar.activation(out=warm[:], in_=warm[:], func=ACT.Tanh)
+        make_identity(nc, ident[:])
+        nc.gpsimd.tensor_copy(out=dx[:], in_=dx_raw[:])
+
+        wide = [keep.tile([P, PACK, H], BF16, name="wide%d" % c, align_bytes=64) for c in range(C)]
+        wi = [keep.tile([P, H, PACK], BF16, name="wi%d" % c, align_bytes=64) for c in range(C)]
+        wc = [keep.tile([P, H], U32, name="wc%d" % c, align_bytes=64) for c in range(C)]
+        ws = [keep.tile([P, H], U8, name="ws%d" % c, align_bytes=64) for c in range(C)]
+
+        def widen(c):
+            for t in range(PACK):
+                src = wb[c][:, t, :].bitcast(FP8)
+                if t < 2 and c == 0:
+                    nc.vector.tensor_scalar(out=wide[c][:, t, :], in0=src, scalar1=wsc[:, t : t + 1], scalar2=None, op0=ALU.mult)
+                else:
+                    nc.scalar.activation(out=wide[c][:, t, :], in_=src, func=ACT.Copy, scale=wsc[:, t : t + 1])
+
+        def interleave_w(c):
+            nc.vector.tensor_copy(out=wi[c][:], in_=wide[c][:].rearrange("p t n -> p n t"))
+
+        def quant_w(c):
+            nc.vector.quantize_mx(out=wc[c][:].bitcast(FP8X4), scales=ws[c][:], in_=wi[c][:].rearrange("p n t -> p (n t)"))
+
+        T1, U1, Q1, F0, ZA, ZB, T2, U2, Q2, MM, F1, PO = ({} for _ in range(12))
+
+        def pair(k):
+            return (2 * k, 2 * k + 1)
+
+        def t1(k):
+            T1[k] = psum.tile([P, 2, 2, P], F32, name="t1", tag="t1", bufs=1)
+            for s, j in enumerate(pair(k)):
+                words = z_tiles[j].bitcast(F32)
+                for u in range(2):
+                    nc.tensor.transpose(T1[k][:, u, s, :], words[:, u : 2 * P : 2], ident[:])
+
+        def a(k):
+            U1[k] = work.tile([P, 2 * P, PACK], BF16, name="u1", tag="u1", align_bytes=64, bufs=3)
+            nc.vector.tensor_tensor(
+                out=U1[k][:].rearrange("p n (u e) -> p n u e", e=2),
+                in0=T1.pop(k)[:].bitcast(BF16).rearrange("p u s (n e) -> p (s n) u e", e=2),
+                in1=gx[:].rearrange("p n (u e) -> p n u e", e=2),
+                op=ALU.mult,
+            )
+
+        def quant(u, name):
+            codes = work.tile([P, 2 * P], U32, name="c" + name, tag="c" + name, align_bytes=64, bufs=3)
+            scales = work.tile([P, 2 * P], U8, name="s" + name, tag="s" + name, align_bytes=64, bufs=3)
+            nc.vector.quantize_mx(out=codes[:].bitcast(FP8X4), scales=scales[:], in_=u[:].rearrange("p n t -> p (n t)"))
+            return codes, scales
+
+        def mm(q, k, stage, order):
+            codes, scales = q
+            for s, c in order:
+                acc = psum.tile([P, H], F32, name="mm", tag="mm", bufs=5)
+                cols = slice(s * P, (s + 1) * P)
+                nc.tensor.matmul_mx(
+                    out=acc[:], lhsT=codes[:, cols].bitcast(FP8X4), lhsT_scale=scales[:, cols],
+                    rhs=wc[c][:].bitcast(FP8X4), rhs_scale=ws[c][:], start=True, stop=True,
+                )
+                MM[2 * k + s, stage, c] = acc
+
+        def tanh1(k, order):
+            for s, c in order:
+                j = 2 * k + s
+                F0[j, c] = work.tile([P, PACK, P], F32, name="f0%d" % c, tag="f0%d" % c)
+                nc.scalar.activation(out=F0[j, c][:], in_=MM.pop((j, 1, c))[:].rearrange("p (m t) -> p t m", t=PACK), func=ACT.Tanh)
+            for j in pair(k):
+                if ts_on_scalar(j):
+                    ZB[j] = work.tile([P, PACK, P], F32, name="zb", tag="zb")
+                    nc.scalar.activation(out=ZB[j][:], in_=F0.pop((j, 1))[:], func=ACT.Copy, scale=dx[:, 0, 2 * j + 1 : 2 * j + 2])
+
+        def tanh2(k, order):
+            for s, c in order:
+                j = 2 * k + s
+                F1[j, c] = work.tile([P, H], F32, name="f1%d" % c, tag="f1%d" % c)
+                nc.scalar.activation(out=F1[j, c][:], in_=MM.pop((j, 2, c))[:], func=ACT.Tanh)
+
+        def ts_on_scalar(j):
+            return j % 4 == 1
+
+        def mid(j):
+            ZA[j] = work.tile([P, PACK, P], F32, name="za", tag="za")
+            nc.vector.scalar_tensor_tensor(
+                out=ZA[j][:], in0=F0.pop((j, 0))[:], scalar=dx[:, 0, 2 * j : 2 * j + 1],
+                in1=z_tiles[j].rearrange("p (m t) -> p t m", t=PACK), op0=ALU.mult, op1=ALU.add,
+            )
+            if not ts_on_scalar(j):
+                ZB[j] = work.tile([P, PACK, P], F32, name="zb", tag="zb")
+                nc.vector.tensor_scalar(out=ZB[j][:], in0=F0.pop((j, 1))[:], scalar1=dx[:, 0, 2 * j + 1 : 2 * j + 2], scalar2=None, op0=ALU.mult)
+
+        def t2(j):
+            T2[j] = psum.tile([P, PACK, P], F32, name="t2", tag="t2", bufs=2)
+            za, zb = ZA.pop(j), ZB.pop(j)
+            for t in range(PACK):
+                nc.tensor.matmul(T2[j][:, t, :], lhsT=za[:, t, :], rhs=ident[:], is_transpose=True, start=True, stop=False)
+                nc.tensor.matmul(T2[j][:, t, :], lhsT=zb[:, t, :], rhs=ident[:], is_transpose=True, start=False, stop=True)
+
+        def d(k):
+            U2[k] = work.tile([P, 2 * P, PACK], BF16, name="u2", tag="u2", align_bytes=64, bufs=3)
+            for s, j in enumerate(pair(k)):
+                nc.vector.tensor_tensor(out=U2[k][:, s * P : (s + 1) * P, :], in0=T2.pop(j)[:].rearrange("p t n -> p n t"), in1=gx[:, 0:P, :], op=ALU.mult)
+
+        def po(k):
+            for j in reversed(pair(k)):
+                PO[j] = work.tile([P, H], F32, name="po%d" % (j % 2), tag="po%d" % (j % 2), bufs=1)
+                nc.gpsimd.tensor_scalar(out=PO[j][:], in0=F1.pop((j, 0))[:], scalar1=dx[:, 1, 2 * j : 2 * j + 1], scalar2=0.0, op0=ALU.mult, op1=ALU.add)
+
+        def fin(k):
+            for j in pair(k):
+                o = work.tile([P, H], F32, name="o", tag="o")
+                nc.vector.scalar_tensor_tensor(
+                    out=o[:], in0=F1.pop((j, 1))[:], scalar=dx[:, 1, 2 * j + 1 : 2 * j + 2], in1=PO.pop(j)[:], op0=ALU.mult, op1=ALU.add,
+                )
+                nc.sync.dma_start(out=out_view[:, j, :], in_=o[:])
+
+        BY_TILE = ((0, 0), (0, 1), (1, 0), (1, 1))
+        BY_CHANNEL = ((0, 0), (1, 0), (0, 1), (1, 1))
+
+        def ok(k):
+            return 0 <= k < GROUPS
+
+        t1(0)
+        widen(0)
+        widen(1)
+        nc.vector.tensor_copy(out=gx[:], in_=g4[:].unsqueeze(1).to_broadcast([P, 2 * P, PACK]))
+        interleave_w(0)
+        a(0)
+        t1(1)
+        quant_w(0)
+        Q1[0] = quant(U1.pop(0), "1")
+        a(1)
+        t1(2)
+        interleave_w(1)
+        Q1[1] = quant(U1.pop(1), "1")
+        quant_w(1)
+        mm(Q1.pop(0), 0, 1, BY_CHANNEL)
+        tanh1(0, BY_CHANNEL)
+        mm(Q1.pop(1), 1, 1, BY_TILE)
+        tanh1(1, BY_TILE)
+
+        for i in range(0, GROUPS + 3):
+            if ok(i - 3):
+                fin(i - 3)
+            if ok(i - 2):
+                po(i - 2)
+            if ok(i - 1):
+                d(i - 1)
+            if ok(i + 2):
+                a(i + 2)
+            if ok(i - 1):
+                Q2[i - 1] = quant(U2.pop(i - 1), "2")
+                mm(Q2.pop(i - 1), i - 1, 2, BY_TILE)
+                tanh2(i - 1, BY_TILE)
+            if ok(i + 2):
+                Q1[i + 2] = quant(U1.pop(i + 2), "1")
+                mm(Q1[i + 2], i + 2, 1, BY_TILE[:1])
+            if ok(i):
+                for j in pair(i):
+                    mid(j)
+                    t2(j)
+            if ok(i + 3):
+                t1(i + 3)
+            if ok(i + 2):
+                mm(Q1.pop(i + 2), i + 2, 1, BY_TILE[1:])
+                tanh1(i + 2, BY_TILE)

@@ -22,6 +22,16 @@ FLOPS = 2 * 2 * B * H * HC
 
 Z_CHUNKS = (2, 2, 4, 8, 8, 8)
 GROUPS = TILES // 2
+TSV = 14
+PRE = 1
+SEQ = [("a", 4, 0), ("d", -1, 0), ("d", -1, 1), ("po", -3, 0), ("po", -3, 1), ("mid", 0, 0), ("q2", -1, 0), ("t1", 5, 0), ("t2", 0, 0), ("m2", -1, 0), ("mid", 0, 1), ("q1", 4, 0), ("t2", 0, 1), ("m2", -1, 1), ("fin", -3, 0), ("fin", -3, 1), ("m1", 3, 0), ("m1", 3, 1)]
+NT1 = 3
+TAILG = 1
+POLAST = 0
+WIDEN_V = (2, 0)
+MMB = 5
+T1B = 1
+FIRST = 4
 
 
 def tile_neuralcdemidpointstep_t_kernel(tc, z0, g, w_bytes, w_scale, dx0, dxm, out):
@@ -33,7 +43,7 @@ def tile_neuralcdemidpointstep_t_kernel(tc, z0, g, w_bytes, w_scale, dx0, dxm, o
     with ExitStack() as ctx:
         ctx.enter_context(tc.manual_schedule())
         keep = ctx.enter_context(tc.tile_pool(name="keep", bufs=1))
-        work = ctx.enter_context(tc.tile_pool(name="work", bufs=6))
+        work = ctx.enter_context(tc.tile_pool(name="work", bufs=10))
         psum = ctx.enter_context(tc.psum_pool(name="psum", bufs=1))
 
         wb = [keep.tile([P, PACK, H], U8, name="wb%d" % c, align_bytes=64) for c in range(C)]
@@ -74,7 +84,7 @@ def tile_neuralcdemidpointstep_t_kernel(tc, z0, g, w_bytes, w_scale, dx0, dxm, o
         def widen(c):
             for t in range(PACK):
                 src = wb[c][:, t, :].bitcast(FP8)
-                if t < 2 and c == 0:
+                if t < WIDEN_V[c]:
                     nc.vector.tensor_scalar(out=wide[c][:, t, :], in0=src, scalar1=wsc[:, t : t + 1], scalar2=None, op0=ALU.mult)
                 else:
                     nc.scalar.activation(out=wide[c][:, t, :], in_=src, func=ACT.Copy, scale=wsc[:, t : t + 1])
@@ -91,7 +101,10 @@ def tile_neuralcdemidpointstep_t_kernel(tc, z0, g, w_bytes, w_scale, dx0, dxm, o
             return (2 * k, 2 * k + 1)
 
         def t1(k):
-            T1[k] = psum.tile([P, 2, 2, P], F32, name="t1", tag="t1", bufs=1)
+            if 0 < k < NT1:
+                T1[k] = psum.tile([P, 2, 2, P], F32, name="t2", tag="t2", bufs=2)
+            else:
+                T1[k] = psum.tile([P, 2, 2, P], F32, name="t1", tag="t1", bufs=T1B)
             for s, j in enumerate(pair(k)):
                 words = z_tiles[j].bitcast(F32)
                 for u in range(2):
@@ -115,7 +128,7 @@ def tile_neuralcdemidpointstep_t_kernel(tc, z0, g, w_bytes, w_scale, dx0, dxm, o
         def mm(q, k, stage, order):
             codes, scales = q
             for s, c in order:
-                acc = psum.tile([P, H], F32, name="mm", tag="mm", bufs=5)
+                acc = psum.tile([P, H], F32, name="mm", tag="mm", bufs=MMB)
                 cols = slice(s * P, (s + 1) * P)
                 nc.tensor.matmul_mx(
                     out=acc[:], lhsT=codes[:, cols].bitcast(FP8X4), lhsT_scale=scales[:, cols],
@@ -128,8 +141,7 @@ def tile_neuralcdemidpointstep_t_kernel(tc, z0, g, w_bytes, w_scale, dx0, dxm, o
                 j = 2 * k + s
                 F0[j, c] = work.tile([P, PACK, P], F32, name="f0%d" % c, tag="f0%d" % c)
                 nc.scalar.activation(out=F0[j, c][:], in_=MM.pop((j, 1, c))[:].rearrange("p (m t) -> p t m", t=PACK), func=ACT.Tanh)
-            for j in pair(k):
-                if ts_on_scalar(j):
+                if c == 1 and ts_on_scalar(j):
                     ZB[j] = work.tile([P, PACK, P], F32, name="zb", tag="zb")
                     nc.scalar.activation(out=ZB[j][:], in_=F0.pop((j, 1))[:], func=ACT.Copy, scale=dx[:, 0, 2 * j + 1 : 2 * j + 2])
 
@@ -140,7 +152,7 @@ def tile_neuralcdemidpointstep_t_kernel(tc, z0, g, w_bytes, w_scale, dx0, dxm, o
                 nc.scalar.activation(out=F1[j, c][:], in_=MM.pop((j, 2, c))[:], func=ACT.Tanh)
 
         def ts_on_scalar(j):
-            return j % 4 == 1
+            return j >= 2 * TSV or (j % 4 == 1 and j // 2 >= PRE)
 
         def mid(j):
             ZA[j] = work.tile([P, PACK, P], F32, name="za", tag="za")
@@ -159,71 +171,109 @@ def tile_neuralcdemidpointstep_t_kernel(tc, z0, g, w_bytes, w_scale, dx0, dxm, o
                 nc.tensor.matmul(T2[j][:, t, :], lhsT=za[:, t, :], rhs=ident[:], is_transpose=True, start=True, stop=False)
                 nc.tensor.matmul(T2[j][:, t, :], lhsT=zb[:, t, :], rhs=ident[:], is_transpose=True, start=False, stop=True)
 
-        def d(k):
-            U2[k] = work.tile([P, 2 * P, PACK], BF16, name="u2", tag="u2", align_bytes=64, bufs=3)
-            for s, j in enumerate(pair(k)):
-                nc.vector.tensor_tensor(out=U2[k][:, s * P : (s + 1) * P, :], in0=T2.pop(j)[:].rearrange("p t n -> p n t"), in1=gx[:, 0:P, :], op=ALU.mult)
+        def d(k, s):
+            if s == 0:
+                U2[k] = work.tile([P, 2 * P, PACK], BF16, name="u2", tag="u2", align_bytes=64, bufs=3)
+            nc.vector.tensor_tensor(out=U2[k][:, s * P : (s + 1) * P, :], in0=T2.pop(2 * k + s)[:].rearrange("p t n -> p n t"), in1=gx[:, 0:P, :], op=ALU.mult)
 
-        def po(k):
-            for j in reversed(pair(k)):
-                PO[j] = work.tile([P, H], F32, name="po%d" % (j % 2), tag="po%d" % (j % 2), bufs=1)
-                nc.gpsimd.tensor_scalar(out=PO[j][:], in0=F1.pop((j, 0))[:], scalar1=dx[:, 1, 2 * j : 2 * j + 1], scalar2=0.0, op0=ALU.mult, op1=ALU.add)
+        def po(j):
+            PO[j] = work.tile([P, H], F32, name="po%d" % (j % 2), tag="po%d" % (j % 2), bufs=1)
+            eng = nc.vector if j >= TILES - POLAST else nc.gpsimd
+            eng.tensor_scalar(out=PO[j][:], in0=F1.pop((j, 0))[:], scalar1=dx[:, 1, 2 * j : 2 * j + 1], scalar2=0.0, op0=ALU.mult, op1=ALU.add)
 
-        def fin(k):
-            for j in pair(k):
-                o = work.tile([P, H], F32, name="o", tag="o")
-                nc.vector.scalar_tensor_tensor(
-                    out=o[:], in0=F1.pop((j, 1))[:], scalar=dx[:, 1, 2 * j + 1 : 2 * j + 2], in1=PO.pop(j)[:], op0=ALU.mult, op1=ALU.add,
-                )
-                nc.sync.dma_start(out=out_view[:, j, :], in_=o[:])
+        def fin(j):
+            o = work.tile([P, H], F32, name="o", tag="o")
+            nc.vector.scalar_tensor_tensor(
+                out=o[:], in0=F1.pop((j, 1))[:], scalar=dx[:, 1, 2 * j + 1 : 2 * j + 2], in1=PO.pop(j)[:], op0=ALU.mult, op1=ALU.add,
+            )
+            nc.sync.dma_start(out=out_view[:, j, :], in_=o[:])
 
-        BY_TILE = ((0, 0), (0, 1), (1, 0), (1, 1))
         BY_CHANNEL = ((0, 0), (1, 0), (0, 1), (1, 1))
+        BY_TILE = ((0, 0), (0, 1), (1, 0), (1, 1))
+        OFF = {(n, s): o for n, o, s in SEQ}
 
         def ok(k):
             return 0 <= k < GROUPS
 
-        t1(0)
+        def m1(k, s):
+            mm(Q1[k], k, 1, BY_TILE[2 * s : 2 * s + 2])
+            tanh1(k, BY_TILE[2 * s : 2 * s + 2])
+
+        def m2(k, s, order=BY_TILE):
+            mm(Q2[k], k, 2, order[2 * s : 2 * s + 2])
+            tanh2(k, order[2 * s : 2 * s + 2])
+
+        for k in range(NT1):
+            t1(k)
         widen(0)
-        widen(1)
         nc.vector.tensor_copy(out=gx[:], in_=g4[:].unsqueeze(1).to_broadcast([P, 2 * P, PACK]))
+        widen(1)
         interleave_w(0)
         a(0)
-        t1(1)
         quant_w(0)
         Q1[0] = quant(U1.pop(0), "1")
+        mm(Q1[0], 0, 1, BY_CHANNEL[:2])
+        tanh1(0, BY_CHANNEL[:2])
+        t1(3)
         a(1)
-        t1(2)
         interleave_w(1)
         Q1[1] = quant(U1.pop(1), "1")
         quant_w(1)
-        mm(Q1.pop(0), 0, 1, BY_CHANNEL)
-        tanh1(0, BY_CHANNEL)
-        mm(Q1.pop(1), 1, 1, BY_TILE)
-        tanh1(1, BY_TILE)
+        mm(Q1[0], 0, 1, BY_CHANNEL[2:])
+        tanh1(0, BY_CHANNEL[2:])
+        a(2)
+        a(3)
+        t1(4)
+        Q1[2] = quant(U1.pop(2), "1")
+        m1(1, 0)
+        m1(1, 1)
+        m1(2, 0)
+        m1(2, 1)
+        Q1[3] = quant(U1.pop(3), "1")
 
-        for i in range(0, GROUPS + 3):
-            if ok(i - 3):
-                fin(i - 3)
-            if ok(i - 2):
-                po(i - 2)
-            if ok(i - 1):
-                d(i - 1)
-            if ok(i + 2):
-                a(i + 2)
-            if ok(i - 1):
-                Q2[i - 1] = quant(U2.pop(i - 1), "2")
-                mm(Q2.pop(i - 1), i - 1, 2, BY_TILE)
-                tanh2(i - 1, BY_TILE)
-            if ok(i + 2):
-                Q1[i + 2] = quant(U1.pop(i + 2), "1")
-                mm(Q1[i + 2], i + 2, 1, BY_TILE[:1])
-            if ok(i):
-                for j in pair(i):
-                    mid(j)
-                    t2(j)
-            if ok(i + 3):
-                t1(i + 3)
-            if ok(i + 2):
-                mm(Q1.pop(i + 2), i + 2, 1, BY_TILE[1:])
-                tanh1(i + 2, BY_TILE)
+        def step(name, k, s):
+            j = 2 * k + s
+            if name == "mid":
+                mid(j)
+            elif name == "t2":
+                t2(j)
+            elif name == "m1":
+                m1(k, s)
+            elif name == "q1":
+                Q1[k] = quant(U1.pop(k), "1")
+            elif name == "t1":
+                t1(k)
+            elif name == "a":
+                a(k)
+            elif name == "d":
+                d(k, s)
+            elif name == "q2":
+                Q2[k] = quant(U2.pop(k), "2")
+            elif name == "m2":
+                m2(k, s)
+            elif name == "po":
+                po(j)
+            elif name == "fin":
+                fin(j)
+
+        for i in range(GROUPS):
+            for name, off, s in SEQ:
+                if ok(i + off):
+                    step(name, i + off, s)
+        po(26)
+        po(27)
+        d(15, 0)
+        d(15, 1)
+        fin(26)
+        Q2[15] = quant(U2.pop(15), "2")
+        m2(15, 0, BY_CHANNEL)
+        fin(27)
+        po(28)
+        po(29)
+        m2(15, 1, BY_CHANNEL)
+        fin(28)
+        fin(29)
+        po(30)
+        po(31)
+        fin(30)
+        fin(31)

@@ -22,12 +22,14 @@ FLOPS = 2 * 2 * B * H * HC
 
 Z_CHUNKS = (2, 2, 4, 8, 8, 8)
 GROUPS = TILES // 2
+ZNUM = 0
+ZDEN = 2
 TSV = 14
 PRE = 1
-SEQ = [("a", 4, 0), ("d", -1, 0), ("d", -1, 1), ("po", -3, 0), ("po", -3, 1), ("mid", 0, 0), ("q2", -1, 0), ("t1", 5, 0), ("t2", 0, 0), ("m2", -1, 0), ("mid", 0, 1), ("q1", 4, 0), ("t2", 0, 1), ("m2", -1, 1), ("fin", -3, 0), ("fin", -3, 1), ("m1", 3, 0), ("m1", 3, 1)]
+SEQ = [('a', 4, 0), ('t1', 5, 0), ('d', -1, 0), ('m1', 2, 1), ('d', -1, 1), ('mid', 0, 0), ('t2', 0, 0), ('mid', 0, 1), ('po', -3, 0), ('po', -3, 1), ('q2', -1, 0), ('q1', 4, 0), ('t2', 0, 1), ('m2', -1, 0), ('fin', -3, 0), ('m2', -1, 1), ('fin', -3, 1), ('m1', 3, 0)]
 NT1 = 3
 TAILG = 1
-POLAST = 0
+POLAST = 4
 WIDEN_V = (2, 0)
 MMB = 5
 T1B = 1
@@ -53,6 +55,7 @@ def tile_neuralcdemidpointstep_t_kernel(tc, z0, g, w_bytes, w_scale, dx0, dxm, o
         dx_raw = keep.tile([P, 2, TILES * C], BF16, name="dx_raw")
         dx = keep.tile([P, 2, TILES * C], F32, name="dx")
         ident = keep.tile([P, P], F32, name="ident")
+        ident16 = keep.tile([P, P], BF16, name="ident16")
         warm = keep.tile([P, 1], F32, name="warm")
 
         z_tiles = {}
@@ -74,6 +77,7 @@ def tile_neuralcdemidpointstep_t_kernel(tc, z0, g, w_bytes, w_scale, dx0, dxm, o
         nc.vector.memset(warm[:], 0.0)
         nc.scalar.activation(out=warm[:], in_=warm[:], func=ACT.Tanh)
         make_identity(nc, ident[:])
+        nc.gpsimd.tensor_copy(out=ident16[:], in_=ident[:])
         nc.gpsimd.tensor_copy(out=dx[:], in_=dx_raw[:])
 
         wide = [keep.tile([P, PACK, H], BF16, name="wide%d" % c, align_bytes=64) for c in range(C)]
@@ -154,12 +158,18 @@ def tile_neuralcdemidpointstep_t_kernel(tc, z0, g, w_bytes, w_scale, dx0, dxm, o
         def ts_on_scalar(j):
             return j >= 2 * TSV or (j % 4 == 1 and j // 2 >= PRE)
 
+        def z_on_pe(j):
+            return j % ZDEN < ZNUM
+
         def mid(j):
             ZA[j] = work.tile([P, PACK, P], F32, name="za", tag="za")
-            nc.vector.scalar_tensor_tensor(
-                out=ZA[j][:], in0=F0.pop((j, 0))[:], scalar=dx[:, 0, 2 * j : 2 * j + 1],
-                in1=z_tiles[j].rearrange("p (m t) -> p t m", t=PACK), op0=ALU.mult, op1=ALU.add,
-            )
+            if z_on_pe(j):
+                nc.vector.tensor_scalar(out=ZA[j][:], in0=F0.pop((j, 0))[:], scalar1=dx[:, 0, 2 * j : 2 * j + 1], scalar2=None, op0=ALU.mult)
+            else:
+                nc.vector.scalar_tensor_tensor(
+                    out=ZA[j][:], in0=F0.pop((j, 0))[:], scalar=dx[:, 0, 2 * j : 2 * j + 1],
+                    in1=z_tiles[j].rearrange("p (m t) -> p t m", t=PACK), op0=ALU.mult, op1=ALU.add,
+                )
             if not ts_on_scalar(j):
                 ZB[j] = work.tile([P, PACK, P], F32, name="zb", tag="zb")
                 nc.vector.tensor_scalar(out=ZB[j][:], in0=F0.pop((j, 1))[:], scalar1=dx[:, 0, 2 * j + 1 : 2 * j + 2], scalar2=None, op0=ALU.mult)
@@ -167,9 +177,15 @@ def tile_neuralcdemidpointstep_t_kernel(tc, z0, g, w_bytes, w_scale, dx0, dxm, o
         def t2(j):
             T2[j] = psum.tile([P, PACK, P], F32, name="t2", tag="t2", bufs=2)
             za, zb = ZA.pop(j), ZB.pop(j)
+            opened = z_on_pe(j)
+            if opened:
+                zt = z_tiles[j].rearrange("p (m t) -> p t m", t=PACK)
+                for t in range(PACK):
+                    nc.tensor.matmul(T2[j][:, t, :], lhsT=zt[:, t, :], rhs=ident16[:], start=(t == 0), stop=False)
             for t in range(PACK):
-                nc.tensor.matmul(T2[j][:, t, :], lhsT=za[:, t, :], rhs=ident[:], is_transpose=True, start=True, stop=False)
-                nc.tensor.matmul(T2[j][:, t, :], lhsT=zb[:, t, :], rhs=ident[:], is_transpose=True, start=False, stop=True)
+                nc.tensor.matmul(T2[j][:, t, :], lhsT=za[:, t, :], rhs=ident[:], is_transpose=True, start=(not opened and t == 0), stop=False)
+            for t in range(PACK):
+                nc.tensor.matmul(T2[j][:, t, :], lhsT=zb[:, t, :], rhs=ident[:], is_transpose=True, start=False, stop=(t == PACK - 1))
 
         def d(k, s):
             if s == 0:
@@ -228,7 +244,8 @@ def tile_neuralcdemidpointstep_t_kernel(tc, z0, g, w_bytes, w_scale, dx0, dxm, o
         m1(1, 0)
         m1(1, 1)
         m1(2, 0)
-        m1(2, 1)
+        if OFF["m1", 1] > 2:
+            m1(2, 1)
         Q1[3] = quant(U1.pop(3), "1")
 
         def step(name, k, s):

from contextlib import ExitStack

import concourse.mybir as mybir
from concourse.masks import make_identity

B, H, C = 4096, 512, 2
HC = C * H
P = 128
PACK = 4
TILES = B // P

F32 = mybir.dt.float32
BF16 = mybir.dt.bfloat16
U32 = mybir.dt.uint32
U8 = mybir.dt.uint8
FP8 = mybir.dt.float8_e4m3fn
FP8X4 = mybir.dt.float8_e4m3fn_x4
ALU = mybir.AluOpType
ACT = mybir.ActivationFunctionType

FLOPS = 2 * 2 * B * H * HC

Z_CHUNKS = (2, 2, 4, 8, 8, 8)
GROUPS = TILES // 2
ZNUM = 0
ZDEN = 2
TSV = 14
PRE = 1
SEQ = [('a', 4, 0), ('t1', 5, 0), ('d', -1, 0), ('m1', 2, 1), ('d', -1, 1), ('mid', 0, 0), ('t2', 0, 0), ('mid', 0, 1), ('po', -3, 0), ('po', -3, 1), ('q2', -1, 0), ('q1', 4, 0), ('t2', 0, 1), ('m2', -1, 0), ('fin', -3, 0), ('m2', -1, 1), ('fin', -3, 1), ('m1', 3, 0)]
NT1 = 3
TAILG = 1
POLAST = 4
WIDEN_V = (2, 0)
MMB = 5
T1B = 1
FIRST = 4


def tile_neuralcdemidpointstep_t_kernel(tc, z0, g, w_bytes, w_scale, dx0, dxm, out):
    nc = tc.nc
    z_view = z0.rearrange("(p j) h -> p j h", j=TILES)
    out_view = out.rearrange("(p j) h -> p j h", j=TILES)
    wb_view = w_bytes.rearrange("(p t) n -> p t n", t=PACK)

    with ExitStack() as ctx:
        ctx.enter_context(tc.manual_schedule())
        keep = ctx.enter_context(tc.tile_pool(name="keep", bufs=1))
        work = ctx.enter_context(tc.tile_pool(name="work", bufs=10))
        psum = ctx.enter_context(tc.psum_pool(name="psum", bufs=1))

        wb = [keep.tile([P, PACK, H], U8, name="wb%d" % c, align_bytes=64) for c in range(C)]
        wsc = keep.tile([P, PACK], F32, name="wsc")
        g4 = keep.tile([P, PACK], BF16, name="g4")
        gx = keep.tile([P, 2 * P, PACK], BF16, name="gx", align_bytes=64)
        dx_raw = keep.tile([P, 2, TILES * C], BF16, name="dx_raw")
        dx = keep.tile([P, 2, TILES * C], F32, name="dx")
        ident = keep.tile([P, P], F32, name="ident")
        ident16 = keep.tile([P, P], BF16, name="ident16")
        warm = keep.tile([P, 1], F32, name="warm")

        z_tiles = {}
        nc.sync.dma_start(out=wb[0][:], in_=wb_view[:, :, 0:H])
        nc.scalar.dma_start(out=wsc[:], in_=w_scale.rearrange("(p t) o -> p (t o)", t=PACK))
        nc.scalar.dma_start(out=g4[:], in_=g.rearrange("(p t) -> p t", t=PACK))
        nc.scalar.dma_start(out=dx_raw[:, 0, :], in_=dx0.rearrange("(p j) c -> p (j c)", j=TILES))
        nc.scalar.dma_start(out=dx_raw[:, 1, :], in_=dxm.rearrange("(p j) c -> p (j c)", j=TILES))
        j0 = 0
        for k, n in enumerate(Z_CHUNKS):
            zc = keep.tile([P, n, H], BF16, name="z%d" % k, align_bytes=64)
            nc.sync.dma_start(out=zc[:], in_=z_view[:, j0 : j0 + n, :])
            for i in range(n):
                z_tiles[j0 + i] = zc[:, i, :]
            j0 += n
            if k == 0:
                nc.sync.dma_start(out=wb[1][:], in_=wb_view[:, :, H:HC])

        nc.vector.memset(warm[:], 0.0)
        nc.scalar.activation(out=warm[:], in_=warm[:], func=ACT.Tanh)
        make_identity(nc, ident[:])
        nc.gpsimd.tensor_copy(out=ident16[:], in_=ident[:])
        nc.gpsimd.tensor_copy(out=dx[:], in_=dx_raw[:])

        wide = [keep.tile([P, PACK, H], BF16, name="wide%d" % c, align_bytes=64) for c in range(C)]
        wi = [keep.tile([P, H, PACK], BF16, name="wi%d" % c, align_bytes=64) for c in range(C)]
        wc = [keep.tile([P, H], U32, name="wc%d" % c, align_bytes=64) for c in range(C)]
        ws = [keep.tile([P, H], U8, name="ws%d" % c, align_bytes=64) for c in range(C)]

        def widen(c):
            for t in range(PACK):
                src = wb[c][:, t, :].bitcast(FP8)
                if t < WIDEN_V[c]:
                    nc.vector.tensor_scalar(out=wide[c][:, t, :], in0=src, scalar1=wsc[:, t : t + 1], scalar2=None, op0=ALU.mult)
                else:
                    nc.scalar.activation(out=wide[c][:, t, :], in_=src, func=ACT.Copy, scale=wsc[:, t : t + 1])

        def interleave_w(c):
            nc.vector.tensor_copy(out=wi[c][:], in_=wide[c][:].rearrange("p t n -> p n t"))

        def quant_w(c):
            nc.vector.quantize_mx(out=wc[c][:].bitcast(FP8X4), scales=ws[c][:], in_=wi[c][:].rearrange("p n t -> p (n t)"))

        T1, U1, Q1, F0, ZA, ZB, T2, U2, Q2, MM, F1, PO = ({} for _ in range(12))

        def pair(k):
            return (2 * k, 2 * k + 1)

        def t1(k):
            if 0 < k < NT1:
                T1[k] = psum.tile([P, 2, 2, P], F32, name="t2", tag="t2", bufs=2)
            else:
                T1[k] = psum.tile([P, 2, 2, P], F32, name="t1", tag="t1", bufs=T1B)
            for s, j in enumerate(pair(k)):
                words = z_tiles[j].bitcast(F32)
                for u in range(2):
                    nc.tensor.transpose(T1[k][:, u, s, :], words[:, u : 2 * P : 2], ident[:])

        def a(k):
            U1[k] = work.tile([P, 2 * P, PACK], BF16, name="u1", tag="u1", align_bytes=64, bufs=3)
            nc.vector.tensor_tensor(
                out=U1[k][:].rearrange("p n (u e) -> p n u e", e=2),
                in0=T1.pop(k)[:].bitcast(BF16).rearrange("p u s (n e) -> p (s n) u e", e=2),
                in1=gx[:].rearrange("p n (u e) -> p n u e", e=2),
                op=ALU.mult,
            )

        def quant(u, name):
            codes = work.tile([P, 2 * P], U32, name="c" + name, tag="c" + name, align_bytes=64, bufs=3)
            scales = work.tile([P, 2 * P], U8, name="s" + name, tag="s" + name, align_bytes=64, bufs=3)
            nc.vector.quantize_mx(out=codes[:].bitcast(FP8X4), scales=scales[:], in_=u[:].rearrange("p n t -> p (n t)"))
            return codes, scales

        def mm(q, k, stage, order):
            codes, scales = q
            for s, c in order:
                acc = psum.tile([P, H], F32, name="mm", tag="mm", bufs=MMB)
                cols = slice(s * P, (s + 1) * P)
                nc.tensor.matmul_mx(
                    out=acc[:], lhsT=codes[:, cols].bitcast(FP8X4), lhsT_scale=scales[:, cols],
                    rhs=wc[c][:].bitcast(FP8X4), rhs_scale=ws[c][:], start=True, stop=True,
                )
                MM[2 * k + s, stage, c] = acc

        def tanh1(k, order):
            for s, c in order:
                j = 2 * k + s
                F0[j, c] = work.tile([P, PACK, P], F32, name="f0%d" % c, tag="f0%d" % c)
                nc.scalar.activation(out=F0[j, c][:], in_=MM.pop((j, 1, c))[:].rearrange("p (m t) -> p t m", t=PACK), func=ACT.Tanh)
                if c == 1 and ts_on_scalar(j):
                    ZB[j] = work.tile([P, PACK, P], F32, name="zb", tag="zb")
                    nc.scalar.activation(out=ZB[j][:], in_=F0.pop((j, 1))[:], func=ACT.Copy, scale=dx[:, 0, 2 * j + 1 : 2 * j + 2])

        def tanh2(k, order):
            for s, c in order:
                j = 2 * k + s
                F1[j, c] = work.tile([P, H], F32, name="f1%d" % c, tag="f1%d" % c)
                nc.scalar.activation(out=F1[j, c][:], in_=MM.pop((j, 2, c))[:], func=ACT.Tanh)

        def ts_on_scalar(j):
            return j >= 2 * TSV or (j % 4 == 1 and j // 2 >= PRE)

        def z_on_pe(j):
            return j % ZDEN < ZNUM

        def mid(j):
            ZA[j] = work.tile([P, PACK, P], F32, name="za", tag="za")
            if z_on_pe(j):
                nc.vector.tensor_scalar(out=ZA[j][:], in0=F0.pop((j, 0))[:], scalar1=dx[:, 0, 2 * j : 2 * j + 1], scalar2=None, op0=ALU.mult)
            else:
                nc.vector.scalar_tensor_tensor(
                    out=ZA[j][:], in0=F0.pop((j, 0))[:], scalar=dx[:, 0, 2 * j : 2 * j + 1],
                    in1=z_tiles[j].rearrange("p (m t) -> p t m", t=PACK), op0=ALU.mult, op1=ALU.add,
                )
            if not ts_on_scalar(j):
                ZB[j] = work.tile([P, PACK, P], F32, name="zb", tag="zb")
                nc.vector.tensor_scalar(out=ZB[j][:], in0=F0.pop((j, 1))[:], scalar1=dx[:, 0, 2 * j + 1 : 2 * j + 2], scalar2=None, op0=ALU.mult)

        def t2(j):
            T2[j] = psum.tile([P, PACK, P], F32, name="t2", tag="t2", bufs=2)
            za, zb = ZA.pop(j), ZB.pop(j)
            opened = z_on_pe(j)
            if opened:
                zt = z_tiles[j].rearrange("p (m t) -> p t m", t=PACK)
                for t in range(PACK):
                    nc.tensor.matmul(T2[j][:, t, :], lhsT=zt[:, t, :], rhs=ident16[:], start=(t == 0), stop=False)
            for t in range(PACK):
                nc.tensor.matmul(T2[j][:, t, :], lhsT=za[:, t, :], rhs=ident[:], is_transpose=True, start=(not opened and t == 0), stop=False)
            for t in range(PACK):
                nc.tensor.matmul(T2[j][:, t, :], lhsT=zb[:, t, :], rhs=ident[:], is_transpose=True, start=False, stop=(t == PACK - 1))

        def d(k, s):
            if s == 0:
                U2[k] = work.tile([P, 2 * P, PACK], BF16, name="u2", tag="u2", align_bytes=64, bufs=3)
            nc.vector.tensor_tensor(out=U2[k][:, s * P : (s + 1) * P, :], in0=T2.pop(2 * k + s)[:].rearrange("p t n -> p n t"), in1=gx[:, 0:P, :], op=ALU.mult)

        def po(j):
            PO[j] = work.tile([P, H], F32, name="po%d" % (j % 2), tag="po%d" % (j % 2), bufs=1)
            eng = nc.vector if j >= TILES - POLAST else nc.gpsimd
            eng.tensor_scalar(out=PO[j][:], in0=F1.pop((j, 0))[:], scalar1=dx[:, 1, 2 * j : 2 * j + 1], scalar2=0.0, op0=ALU.mult, op1=ALU.add)

        def fin(j):
            o = work.tile([P, H], F32, name="o", tag="o")
            nc.vector.scalar_tensor_tensor(
                out=o[:], in0=F1.pop((j, 1))[:], scalar=dx[:, 1, 2 * j + 1 : 2 * j + 2], in1=PO.pop(j)[:], op0=ALU.mult, op1=ALU.add,
            )
            nc.sync.dma_start(out=out_view[:, j, :], in_=o[:])

        BY_CHANNEL = ((0, 0), (1, 0), (0, 1), (1, 1))
        BY_TILE = ((0, 0), (0, 1), (1, 0), (1, 1))
        OFF = {(n, s): o for n, o, s in SEQ}

        def ok(k):
            return 0 <= k < GROUPS

        def m1(k, s):
            mm(Q1[k], k, 1, BY_TILE[2 * s : 2 * s + 2])
            tanh1(k, BY_TILE[2 * s : 2 * s + 2])

        def m2(k, s, order=BY_TILE):
            mm(Q2[k], k, 2, order[2 * s : 2 * s + 2])
            tanh2(k, order[2 * s : 2 * s + 2])

        for k in range(NT1):
            t1(k)
        widen(0)
        nc.vector.tensor_copy(out=gx[:], in_=g4[:].unsqueeze(1).to_broadcast([P, 2 * P, PACK]))
        widen(1)
        interleave_w(0)
        a(0)
        quant_w(0)
        Q1[0] = quant(U1.pop(0), "1")
        mm(Q1[0], 0, 1, BY_CHANNEL[:2])
        tanh1(0, BY_CHANNEL[:2])
        t1(3)
        a(1)
        interleave_w(1)
        Q1[1] = quant(U1.pop(1), "1")
        quant_w(1)
        mm(Q1[0], 0, 1, BY_CHANNEL[2:])
        tanh1(0, BY_CHANNEL[2:])
        a(2)
        a(3)
        t1(4)
        Q1[2] = quant(U1.pop(2), "1")
        m1(1, 0)
        m1(1, 1)
        m1(2, 0)
        if OFF["m1", 1] > 2:
            m1(2, 1)
        Q1[3] = quant(U1.pop(3), "1")

        def step(name, k, s):
            j = 2 * k + s
            if name == "mid":
                mid(j)
            elif name == "t2":
                t2(j)
            elif name == "m1":
                m1(k, s)
            elif name == "q1":
                Q1[k] = quant(U1.pop(k), "1")
            elif name == "t1":
                t1(k)
            elif name == "a":
                a(k)
            elif name == "d":
                d(k, s)
            elif name == "q2":
                Q2[k] = quant(U2.pop(k), "2")
            elif name == "m2":
                m2(k, s)
            elif name == "po":
                po(j)
            elif name == "fin":
                fin(j)

        for i in range(GROUPS):
            for name, off, s in SEQ:
                if ok(i + off):
                    step(name, i + off, s)
        po(26)
        po(27)
        d(15, 0)
        d(15, 1)
        fin(26)
        Q2[15] = quant(U2.pop(15), "2")
        m2(15, 0, BY_CHANNEL)
        fin(27)
        po(28)
        po(29)
        m2(15, 1, BY_CHANNEL)
        fin(28)
        fin(29)
        po(30)
        po(31)
        fin(30)
        fin(31)
